import numpy as np
import ml_dtypes

BF16 = ml_dtypes.bfloat16


def bf(x):
    return np.asarray(x, np.float32).astype(BF16)


def f32(x):
    return np.asarray(x, np.float32)


def f64(x):
    return np.asarray(x).astype(np.float64)


def striped(idx):
    return np.tile(idx.reshape(-1, 16).T, (8, 1))


S, K, M, N, E, Q = 256, 256, 128, 256, 4, 64


def sigmoid(v):
    return 1.0 / (1.0 + np.exp(-v))


def setup_inputs():
    return {"table": bf(np.random.standard_normal((S, K))), "w": bf(np.random.standard_normal((E, K, M)) / np.sqrt(K)), "b": f32(0.5 * np.random.standard_normal((M, 1))), "offs": striped(np.sort(np.random.permutation(S).reshape(E, Q), axis=1).reshape(-1))}


def reference(table, w, b, offs):
    idx = offs[:16].T.reshape(-1)
    x = f64(table)[idx].T
    y = np.concatenate([f64(w)[e].T @ x[:, e * Q : (e + 1) * Q] for e in range(E)], axis=1)
    return (y + f64(b)) * sigmoid(y + f64(b))

@@ -1,0 +1,88 @@
+import concourse.mybir as mybir
+from concourse.masks import make_identity
+
+BF16, F32, U16 = mybir.dt.bfloat16, mybir.dt.float32, mybir.dt.uint16
+SILU = mybir.ActivationFunctionType.Silu
+
+P = 128
+TOKENS = 256
+FEATURES = 256
+OUT_FEATURES = 128
+EXPERTS = 4
+PIECE = 64
+ENTRIES = EXPERTS * PIECE
+TOKEN_BLOCKS = TOKENS // P
+FEATURE_BLOCKS = FEATURES // P
+PIECE_COLUMNS = PIECE // 16
+HALVES = 2
+HALF_EXPERTS = EXPERTS // HALVES
+HALF_ENTRIES = ENTRIES // HALVES
+BANK_COLUMNS = 512
+WARMING_MATMULS = 3
+
+FLOPS = 2 * FEATURES * OUT_FEATURES * ENTRIES
+
+
+def tile_gather_matmul_kernel(tc, table, w, b, offs, out):
+    nc = tc.nc
+    with tc.tile_pool(name="held", bufs=1) as held, tc.psum_pool(name="psum", bufs=1) as psum:
+        token_rows = [held.tile([P, FEATURES], BF16, name=f"token_rows{t}") for t in range(TOKEN_BLOCKS)]
+        nc.sync.dma_start(token_rows[0][:], table[0:P, :])
+        nc.scalar.dma_start(token_rows[1][:], table[P : 2 * P, :])
+
+        offsets = held.tile([P, ENTRIES // 16], U16, name="offsets")
+        nc.sync.dma_start(offsets[:], offs)
+
+        weights = held.tile([P, EXPERTS * FEATURE_BLOCKS, OUT_FEATURES], BF16, name="weights")
+        w_blocks = w.flatten_outer_dims().rearrange("(c p) m -> p c m", p=P)
+        half = EXPERTS * FEATURE_BLOCKS // 2
+        nc.sync.dma_start(weights[:, 0:half, :], w_blocks[:, 0:half, :])
+        nc.scalar.dma_start(weights[:, half:, :], w_blocks[:, half:, :])
+
+        bias = held.tile([P, 1], F32, name="bias")
+        nc.sync.dma_start(bias[:], b)
+
+        zeros_f32 = held.tile([P, BANK_COLUMNS // 2], F32, name="zeros_f32")
+        nc.vector.memset(zeros_f32[:], 0.0)
+        zeros = zeros_f32[:].bitcast(BF16)
+
+        unread_product = psum.tile([P, BANK_COLUMNS], F32, name="unread_product")
+        for i in range(WARMING_MATMULS):
+            nc.tensor.matmul(unread_product[:], zeros[:, 0:P], zeros, start=True, stop=True)
+
+        unread_silu = held.tile([P, 1], F32, name="unread_silu")
+        nc.scalar.activation(unread_silu[:], zeros[:, 0:1], SILU)
+
+        identity = held.tile([P, P], BF16, name="identity")
+        make_identity(nc, identity[:])
+
+        windows = []
+        for f in range(FEATURE_BLOCKS):
+            flipped = psum.tile([P, TOKENS], BF16, name=f"flipped{f}")
+            for t in range(TOKEN_BLOCKS):
+                nc.tensor.transpose(
+                    flipped[:, t * P : (t + 1) * P], token_rows[t][:, f * P : (f + 1) * P], identity[:]
+                )
+            window = held.tile([P, TOKENS], BF16, name=f"window{f}")
+            if f % 2 == 0:
+                nc.vector.tensor_copy(window[:], flipped[:])
+            else:
+                nc.scalar.copy(window[:], flipped[:])
+            windows.append(window)
+
+        for h in range(HALVES):
+            product = psum.tile([P, HALF_ENTRIES], F32, name=f"product{h}")
+            for i in range(HALF_EXPERTS):
+                e = h * HALF_EXPERTS + i
+                piece = offsets[:, e * PIECE_COLUMNS : (e + 1) * PIECE_COLUMNS]
+                for f in range(FEATURE_BLOCKS):
+                    nc.tensor.matmul(
+                        product[:, i * PIECE : (i + 1) * PIECE],
+                        weights[:, e * FEATURE_BLOCKS + f, :],
+                        windows[f][:].indirect(piece),
+                        start=(f == 0),
+                        stop=(f == FEATURE_BLOCKS - 1),
+                    )
+            result = held.tile([P, HALF_ENTRIES], F32, name=f"result{h}")
+            nc.scalar.activation(result[:], product[:], SILU, bias=bias[:, 0:1])
+            nc.sync.dma_start(out[:, h * HALF_ENTRIES : (h + 1) * HALF_ENTRIES], result[:])

@@ -70,19 +70,19 @@ def tile_gather_matmul_kernel(tc, table, w, b, offs, out):
                 nc.scalar.copy(window[:], flipped[:])
             windows.append(window)
 
+        products = [psum.tile([P, HALF_ENTRIES], F32, name=f"product{h}") for h in range(HALVES)]
+        for f in range(FEATURE_BLOCKS):
+            for e in range(EXPERTS):
+                h, place = divmod(e, HALF_EXPERTS)
+                nc.tensor.matmul(
+                    products[h][:, place * PIECE : (place + 1) * PIECE],
+                    weights[:, e * FEATURE_BLOCKS + f, :],
+                    windows[f][:].indirect(offsets[:, e * PIECE_COLUMNS : (e + 1) * PIECE_COLUMNS]),
+                    start=(f == 0 and place == 0),
+                    stop=(f == FEATURE_BLOCKS - 1 and place == HALF_EXPERTS - 1),
+                )
+
         for h in range(HALVES):
-            product = psum.tile([P, HALF_ENTRIES], F32, name=f"product{h}")
-            for i in range(HALF_EXPERTS):
-                e = h * HALF_EXPERTS + i
-                piece = offsets[:, e * PIECE_COLUMNS : (e + 1) * PIECE_COLUMNS]
-                for f in range(FEATURE_BLOCKS):
-                    nc.tensor.matmul(
-                        product[:, i * PIECE : (i + 1) * PIECE],
-                        weights[:, e * FEATURE_BLOCKS + f, :],
-                        windows[f][:].indirect(piece),
-                        start=(f == 0),
-                        stop=(f == FEATURE_BLOCKS - 1),
-                    )
             result = held.tile([P, HALF_ENTRIES], F32, name=f"result{h}")
-            nc.scalar.activation(result[:], product[:], SILU, bias=bias[:, 0:1])
+            nc.scalar.activation(result[:], products[h][:], SILU, bias=bias[:, 0:1])
             nc.sync.dma_start(out[:, h * HALF_ENTRIES : (h + 1) * HALF_ENTRIES], result[:])

@@ -33,11 +33,10 @@ def tile_gather_matmul_kernel(tc, table, w, b, offs, out):
         offsets = held.tile([P, ENTRIES // 16], U16, name="offsets")
         nc.sync.dma_start(offsets[:], offs)
 
-        weights = held.tile([P, EXPERTS * FEATURE_BLOCKS, OUT_FEATURES], BF16, name="weights")
-        w_blocks = w.flatten_outer_dims().rearrange("(c p) m -> p c m", p=P)
-        half = EXPERTS * FEATURE_BLOCKS // 2
-        nc.sync.dma_start(weights[:, 0:half, :], w_blocks[:, 0:half, :])
-        nc.scalar.dma_start(weights[:, half:, :], w_blocks[:, half:, :])
+        weights = held.tile([P, EXPERTS, FEATURE_BLOCKS, OUT_FEATURES], BF16, name="weights")
+        w_row_pairs = w.rearrange("e (p f) m -> p e f m", f=FEATURE_BLOCKS)
+        nc.sync.dma_start(weights[:, 0:HALF_EXPERTS], w_row_pairs[:, 0:HALF_EXPERTS])
+        nc.scalar.dma_start(weights[:, HALF_EXPERTS:], w_row_pairs[:, HALF_EXPERTS:])
 
         bias = held.tile([P, 1], F32, name="bias")
         nc.sync.dma_start(bias[:], b)
@@ -56,19 +55,15 @@ def tile_gather_matmul_kernel(tc, table, w, b, offs, out):
         identity = held.tile([P, P], BF16, name="identity")
         make_identity(nc, identity[:])
 
-        windows = []
+        windows = [held.tile([P, TOKENS], BF16, name=f"window{f}") for f in range(FEATURE_BLOCKS)]
         for f in range(FEATURE_BLOCKS):
-            flipped = psum.tile([P, TOKENS], BF16, name=f"flipped{f}")
             for t in range(TOKEN_BLOCKS):
-                nc.tensor.transpose(
-                    flipped[:, t * P : (t + 1) * P], token_rows[t][:, f * P : (f + 1) * P], identity[:]
-                )
-            window = held.tile([P, TOKENS], BF16, name=f"window{f}")
-            if f % 2 == 0:
-                nc.vector.tensor_copy(window[:], flipped[:])
-            else:
-                nc.scalar.copy(window[:], flipped[:])
-            windows.append(window)
+                flipped = psum.tile([P, P], BF16, name=f"flipped{f}{t}")
+                nc.tensor.transpose(flipped[:], token_rows[t][:, f::FEATURE_BLOCKS], identity[:])
+                if t % 2 == 0:
+                    nc.vector.tensor_copy(windows[f][:, t * P : (t + 1) * P], flipped[:])
+                else:
+                    nc.scalar.copy(windows[f][:, t * P : (t + 1) * P], flipped[:])
 
         products = [psum.tile([P, HALF_ENTRIES], F32, name=f"product{h}") for h in range(HALVES)]
         for f in range(FEATURE_BLOCKS):
@@ -76,7 +71,7 @@ def tile_gather_matmul_kernel(tc, table, w, b, offs, out):
                 h, place = divmod(e, HALF_EXPERTS)
                 nc.tensor.matmul(
                     products[h][:, place * PIECE : (place + 1) * PIECE],
-                    weights[:, e * FEATURE_BLOCKS + f, :],
+                    weights[:, e, f, :],
                     windows[f][:].indirect(offsets[:, e * PIECE_COLUMNS : (e + 1) * PIECE_COLUMNS]),
                     start=(f == 0 and place == 0),
                     stop=(f == FEATURE_BLOCKS - 1 and place == HALF_EXPERTS - 1),

@@ -41,16 +41,24 @@ def tile_gather_matmul_kernel(tc, table, w, b, offs, out):
         bias = held.tile([P, 1], F32, name="bias")
         nc.sync.dma_start(bias[:], b)
 
-        zeros_f32 = held.tile([P, BANK_COLUMNS // 2], F32, name="zeros_f32")
+
+        zero_column = held.tile([P, 1], F32, name="zero_column")
+        nc.vector.memset(zero_column[:], 0.0)
+        unread_silu = held.tile([P, 1], F32, name="unread_silu")
+        nc.scalar.activation(unread_silu[:], zero_column[:], SILU)
+
+        zeros_f32 = held.tile([P, P // 2], F32, name="zeros_f32")
         nc.vector.memset(zeros_f32[:], 0.0)
         zeros = zeros_f32[:].bitcast(BF16)
-
-        unread_product = psum.tile([P, BANK_COLUMNS], F32, name="unread_product")
+        unread_product = psum.tile([P, BANK_COLUMNS // P, P], F32, name="unread_product")
         for i in range(WARMING_MATMULS):
-            nc.tensor.matmul(unread_product[:], zeros[:, 0:P], zeros, start=True, stop=True)
-
-        unread_silu = held.tile([P, 1], F32, name="unread_silu")
-        nc.scalar.activation(unread_silu[:], zeros[:, 0:1], SILU)
+            nc.tensor.matmul(
+                unread_product[:],
+                zeros,
+                zeros.unsqueeze(1).to_broadcast([P, BANK_COLUMNS // P, P]),
+                start=True,
+                stop=True,
+            )
 
         identity = held.tile([P, P], BF16, name="identity")
         make_identity(nc, identity[:])

@@ -48,7 +48,7 @@ def tile_gather_matmul_kernel(tc, table, w, b, offs, out):
         nc.scalar.activation(unread_silu[:], zero_column[:], SILU)
 
         zeros_f32 = held.tile([P, P // 2], F32, name="zeros_f32")
-        nc.vector.memset(zeros_f32[:], 0.0)
+        nc.gpsimd.memset(zeros_f32[:], 0.0)
         zeros = zeros_f32[:].bitcast(BF16)
         unread_product = psum.tile([P, BANK_COLUMNS // P, P], F32, name="unread_product")
         for i in range(WARMING_MATMULS):

@@ -68,10 +68,7 @@ def tile_gather_matmul_kernel(tc, table, w, b, offs, out):
             for t in range(TOKEN_BLOCKS):
                 flipped = psum.tile([P, P], BF16, name=f"flipped{f}{t}")
                 nc.tensor.transpose(flipped[:], token_rows[t][:, f::FEATURE_BLOCKS], identity[:])
-                if t % 2 == 0:
-                    nc.vector.tensor_copy(windows[f][:, t * P : (t + 1) * P], flipped[:])
-                else:
-                    nc.scalar.copy(windows[f][:, t * P : (t + 1) * P], flipped[:])
+                nc.scalar.copy(windows[f][:, t * P : (t + 1) * P], flipped[:])
 
         products = [psum.tile([P, HALF_ENTRIES], F32, name=f"product{h}") for h in range(HALVES)]
         for f in range(FEATURE_BLOCKS):

@@ -71,16 +71,17 @@ def tile_gather_matmul_kernel(tc, table, w, b, offs, out):
                 nc.scalar.copy(windows[f][:, t * P : (t + 1) * P], flipped[:])
 
         products = [psum.tile([P, HALF_ENTRIES], F32, name=f"product{h}") for h in range(HALVES)]
-        for f in range(FEATURE_BLOCKS):
-            for e in range(EXPERTS):
-                h, place = divmod(e, HALF_EXPERTS)
-                nc.tensor.matmul(
-                    products[h][:, place * PIECE : (place + 1) * PIECE],
-                    weights[:, e, f, :],
-                    windows[f][:].indirect(offsets[:, e * PIECE_COLUMNS : (e + 1) * PIECE_COLUMNS]),
-                    start=(f == 0 and place == 0),
-                    stop=(f == FEATURE_BLOCKS - 1 and place == HALF_EXPERTS - 1),
-                )
+        for h in range(HALVES):
+            for f in range(FEATURE_BLOCKS):
+                for place in range(HALF_EXPERTS):
+                    e = h * HALF_EXPERTS + place
+                    nc.tensor.matmul(
+                        products[h][:, place * PIECE : (place + 1) * PIECE],
+                        weights[:, e, f, :],
+                        windows[f][:].indirect(offsets[:, e * PIECE_COLUMNS : (e + 1) * PIECE_COLUMNS]),
+                        start=(f == 0 and place == 0),
+                        stop=(f == FEATURE_BLOCKS - 1 and place == HALF_EXPERTS - 1),
+                    )
 
         for h in range(HALVES):
             result = held.tile([P, HALF_ENTRIES], F32, name=f"result{h}")

@@ -66,11 +66,15 @@ def tile_gather_matmul_kernel(tc, table, w, b, offs, out):
         windows = [held.tile([P, TOKENS], BF16, name=f"window{f}") for f in range(FEATURE_BLOCKS)]
         for f in range(FEATURE_BLOCKS):
             for t in range(TOKEN_BLOCKS):
-                flipped = psum.tile([P, P], BF16, name=f"flipped{f}{t}")
+                flipped = psum.tile([P, P], BF16, name=f"flipped{f}{t}", tag=f"bank{f}{t}")
                 nc.tensor.transpose(flipped[:], token_rows[t][:, f::FEATURE_BLOCKS], identity[:])
                 nc.scalar.copy(windows[f][:, t * P : (t + 1) * P], flipped[:])
 
-        products = [psum.tile([P, HALF_ENTRIES], F32, name=f"product{h}") for h in range(HALVES)]
+        last_flip_bank = f"bank{FEATURE_BLOCKS - 1}{TOKEN_BLOCKS - 1}"
+        products = [
+            psum.tile([P, HALF_ENTRIES], F32, name="product0"),
+            psum.tile([P, HALF_ENTRIES], F32, name="product1", tag=last_flip_bank),
+        ]
         for h in range(HALVES):
             for f in range(FEATURE_BLOCKS):
                 for place in range(HALF_EXPERTS):

@@ -35,8 +35,8 @@ def tile_gather_matmul_kernel(tc, table, w, b, offs, out):
 
         weights = held.tile([P, EXPERTS, FEATURE_BLOCKS, OUT_FEATURES], BF16, name="weights")
         w_row_pairs = w.rearrange("e (p f) m -> p e f m", f=FEATURE_BLOCKS)
-        nc.sync.dma_start(weights[:, 0:HALF_EXPERTS], w_row_pairs[:, 0:HALF_EXPERTS])
-        nc.scalar.dma_start(weights[:, HALF_EXPERTS:], w_row_pairs[:, HALF_EXPERTS:])
+        nc.scalar.dma_start(weights[:, 0:HALF_EXPERTS], w_row_pairs[:, 0:HALF_EXPERTS])
+        nc.sync.dma_start(weights[:, HALF_EXPERTS:], w_row_pairs[:, HALF_EXPERTS:])
 
         bias = held.tile([P, 1], F32, name="bias")
         nc.sync.dma_start(bias[:], b)

@@ -71,23 +71,23 @@ def tile_gather_matmul_kernel(tc, table, w, b, offs, out):
                 nc.scalar.copy(windows[f][:, t * P : (t + 1) * P], flipped[:])
 
         last_flip_bank = f"bank{FEATURE_BLOCKS - 1}{TOKEN_BLOCKS - 1}"
-        products = [
-            psum.tile([P, HALF_ENTRIES], F32, name="product0"),
-            psum.tile([P, HALF_ENTRIES], F32, name="product1", tag=last_flip_bank),
-        ]
+        product_banks = [f"product{e}" for e in range(EXPERTS - 1)] + [last_flip_bank]
+        products = [psum.tile([P, PIECE], F32, name=f"product{e}", tag=product_banks[e]) for e in range(EXPERTS)]
         for h in range(HALVES):
             for f in range(FEATURE_BLOCKS):
-                for place in range(HALF_EXPERTS):
-                    e = h * HALF_EXPERTS + place
+                for e in range(h * HALF_EXPERTS, (h + 1) * HALF_EXPERTS):
                     nc.tensor.matmul(
-                        products[h][:, place * PIECE : (place + 1) * PIECE],
+                        products[e][:],
                         weights[:, e, f, :],
                         windows[f][:].indirect(offsets[:, e * PIECE_COLUMNS : (e + 1) * PIECE_COLUMNS]),
-                        start=(f == 0 and place == 0),
-                        stop=(f == FEATURE_BLOCKS - 1 and place == HALF_EXPERTS - 1),
+                        start=(f == 0),
+                        stop=(f == FEATURE_BLOCKS - 1),
                     )
 
         for h in range(HALVES):
-            result = held.tile([P, HALF_ENTRIES], F32, name=f"result{h}")
-            nc.scalar.activation(result[:], products[h][:], SILU, bias=bias[:, 0:1])
-            nc.sync.dma_start(out[:, h * HALF_ENTRIES : (h + 1) * HALF_ENTRIES], result[:])
+            result = held.tile([P, HALF_EXPERTS, PIECE], F32, name=f"result{h}")
+            for place in range(HALF_EXPERTS):
+                nc.scalar.activation(result[:, place, :], products[h * HALF_EXPERTS + place][:], SILU, bias=bias[:, 0:1])
+            nc.sync.dma_start(
+                out[:, h * HALF_ENTRIES : (h + 1) * HALF_ENTRIES].rearrange("m (e j) -> m e j", j=PIECE), result[:]
+            )

import concourse.mybir as mybir
from concourse.masks import make_identity

BF16, F32, U16 = mybir.dt.bfloat16, mybir.dt.float32, mybir.dt.uint16
SILU = mybir.ActivationFunctionType.Silu

P = 128
TOKENS = 256
FEATURES = 256
OUT_FEATURES = 128
EXPERTS = 4
PIECE = 64
ENTRIES = EXPERTS * PIECE
TOKEN_BLOCKS = TOKENS // P
FEATURE_BLOCKS = FEATURES // P
PIECE_COLUMNS = PIECE // 16
HALVES = 2
HALF_EXPERTS = EXPERTS // HALVES
HALF_ENTRIES = ENTRIES // HALVES
BANK_COLUMNS = 512
WARMING_MATMULS = 3

FLOPS = 2 * FEATURES * OUT_FEATURES * ENTRIES


def tile_gather_matmul_kernel(tc, table, w, b, offs, out):
    nc = tc.nc
    with tc.tile_pool(name="held", bufs=1) as held, tc.psum_pool(name="psum", bufs=1) as psum:
        token_rows = [held.tile([P, FEATURES], BF16, name=f"token_rows{t}") for t in range(TOKEN_BLOCKS)]
        nc.sync.dma_start(token_rows[0][:], table[0:P, :])
        nc.scalar.dma_start(token_rows[1][:], table[P : 2 * P, :])

        offsets = held.tile([P, ENTRIES // 16], U16, name="offsets")
        nc.sync.dma_start(offsets[:], offs)

        weights = held.tile([P, EXPERTS, FEATURE_BLOCKS, OUT_FEATURES], BF16, name="weights")
        w_row_pairs = w.rearrange("e (p f) m -> p e f m", f=FEATURE_BLOCKS)
        nc.scalar.dma_start(weights[:, 0:HALF_EXPERTS], w_row_pairs[:, 0:HALF_EXPERTS])
        nc.sync.dma_start(weights[:, HALF_EXPERTS:], w_row_pairs[:, HALF_EXPERTS:])

        bias = held.tile([P, 1], F32, name="bias")
        nc.sync.dma_start(bias[:], b)


        zero_column = held.tile([P, 1], F32, name="zero_column")
        nc.vector.memset(zero_column[:], 0.0)
        unread_silu = held.tile([P, 1], F32, name="unread_silu")
        nc.scalar.activation(unread_silu[:], zero_column[:], SILU)

        zeros_f32 = held.tile([P, P // 2], F32, name="zeros_f32")
        nc.gpsimd.memset(zeros_f32[:], 0.0)
        zeros = zeros_f32[:].bitcast(BF16)
        unread_product = psum.tile([P, BANK_COLUMNS // P, P], F32, name="unread_product")
        for i in range(WARMING_MATMULS):
            nc.tensor.matmul(
                unread_product[:],
                zeros,
                zeros.unsqueeze(1).to_broadcast([P, BANK_COLUMNS // P, P]),
                start=True,
                stop=True,
            )

        identity = held.tile([P, P], BF16, name="identity")
        make_identity(nc, identity[:])

        windows = [held.tile([P, TOKENS], BF16, name=f"window{f}") for f in range(FEATURE_BLOCKS)]
        for f in range(FEATURE_BLOCKS):
            for t in range(TOKEN_BLOCKS):
                flipped = psum.tile([P, P], BF16, name=f"flipped{f}{t}", tag=f"bank{f}{t}")
                nc.tensor.transpose(flipped[:], token_rows[t][:, f::FEATURE_BLOCKS], identity[:])
                nc.scalar.copy(windows[f][:, t * P : (t + 1) * P], flipped[:])

        last_flip_bank = f"bank{FEATURE_BLOCKS - 1}{TOKEN_BLOCKS - 1}"
        product_banks = [f"product{e}" for e in range(EXPERTS - 1)] + [last_flip_bank]
        products = [psum.tile([P, PIECE], F32, name=f"product{e}", tag=product_banks[e]) for e in range(EXPERTS)]
        for h in range(HALVES):
            for f in range(FEATURE_BLOCKS):
                for e in range(h * HALF_EXPERTS, (h + 1) * HALF_EXPERTS):
                    nc.tensor.matmul(
                        products[e][:],
                        weights[:, e, f, :],
                        windows[f][:].indirect(offsets[:, e * PIECE_COLUMNS : (e + 1) * PIECE_COLUMNS]),
                        start=(f == 0),
                        stop=(f == FEATURE_BLOCKS - 1),
                    )

        for h in range(HALVES):
            result = held.tile([P, HALF_EXPERTS, PIECE], F32, name=f"result{h}")
            for place in range(HALF_EXPERTS):
                nc.scalar.activation(result[:, place, :], products[h * HALF_EXPERTS + place][:], SILU, bias=bias[:, 0:1])
            nc.sync.dma_start(
                out[:, h * HALF_ENTRIES : (h + 1) * HALF_ENTRIES].rearrange("m (e j) -> m e j", j=PIECE), result[:]
            )
